import numpy as np
import ml_dtypes


def mxq(x, axis, fmt="e4m3"):
    dtype, down = {"e4m3": (ml_dtypes.float8_e4m3fn, 7), "e5m2": (ml_dtypes.float8_e5m2, 14)}[fmt]
    v = np.moveaxis(np.asarray(x, np.float32).astype(ml_dtypes.bfloat16).astype(np.float64), axis, -1)
    blocks = v.reshape(v.shape[:-1] + (-1, 32))
    amax = np.abs(blocks).max(-1, keepdims=True)
    byte = np.maximum(np.where(amax > 0, np.frexp(amax)[1] - 1 + 127, 0) - down, 1)
    scale = np.exp2(byte - 127.0)
    codes = (blocks / scale).astype(np.float32).astype(dtype).astype(np.float64)
    return np.moveaxis((codes * scale).reshape(v.shape), -1, axis)


WIDE = False


def mx_kscale(k):
    if not WIDE:
        return np.ones(k)
    levels = np.array([10, -10, 5, -5, 0])
    if k % 512:
        return np.exp2(np.random.permutation(np.resize(levels, k // 32))).repeat(32)
    a = np.empty((k // 512, 16))
    for p in range(k // 512):
        a[p, :8] = np.random.permutation(np.resize(levels, 8))
        for g in range(8):
            far = levels[np.abs(levels - a[p, g]) >= 10]
            a[p, g + 8] = far[np.random.randint(len(far))]
    return np.exp2(a.ravel()).repeat(32)


def f64(x):
    return np.asarray(x).astype(np.float64)


def striped(idx):
    return np.tile(np.asarray(idx).reshape(-1, 16).T, (8, 1)).astype(np.uint16)


def unstriped(offs):
    return offs[:16].T.reshape(-1).astype(np.int64)


E2M1 = np.array([0.0, 0.5, 1.0, 1.5, 2.0, 3.0, 4.0, 6.0, -0.0, -0.5, -1.0, -1.5, -2.0, -3.0, -4.0, -6.0])


def pack_weight(w, fmt):
    k, n = w.shape
    w = f64(np.asarray(w, np.float32).astype(ml_dtypes.bfloat16)).reshape(k // 32, 32, n)
    amax = np.abs(w).max(1)
    if fmt == "e4m3":
        byte = np.frexp(amax)[1] - 1 + 127 - 7
    else:
        mant, ex = np.frexp(amax / 6.0)
        byte = np.where(mant > 0.5, ex, ex - 1) + 127
    byte = np.clip(np.where(amax > 0, byte, 1), 1, 254)
    scaled = (w * np.exp2(127.0 - byte)[:, None, :]).reshape(k, n).astype(np.float32)
    by_word = np.ascontiguousarray(scaled.reshape(k // 512, 128, 4, n).transpose(0, 1, 3, 2))
    if fmt == "e4m3":
        words = by_word.astype(ml_dtypes.float8_e4m3fn).view(np.uint8)
    else:
        c = by_word.astype(ml_dtypes.float4_e2m1fn).view(np.uint8) & 0xF
        words = (c[..., 0::2] | (c[..., 1::2] << 4)).reshape(k // 512, 128, 2 * n)
    return np.ascontiguousarray(words), np.ascontiguousarray(byte.astype(np.uint8).reshape(k // 512, 16, n))


def unpack_weight(words, scales, fmt):
    g, _, n = scales.shape
    words = np.ascontiguousarray(words).reshape(g, 128, n, -1)
    if fmt == "e4m3":
        vals = words.view(ml_dtypes.float8_e4m3fn).astype(np.float64)
    else:
        nib = np.empty((g, 128, n, 4), np.uint8)
        nib[..., 0::2] = words & 0xF
        nib[..., 1::2] = words >> 4
        vals = E2M1[nib]
    vals = vals * np.repeat(np.exp2(scales.astype(np.float64) - 127.0), 8, axis=1)[..., None]
    return vals.transpose(0, 1, 3, 2).reshape(g * 512, n)


K, T, J, N = 1024, 2048, 512, 512


def setup_inputs():
    n = np.random.standard_normal
    idx = np.random.permutation(T)[:J]
    idx2 = np.random.permutation(T)[:J]
    fk = mx_kscale(K)
    xtp = pack_weight(n((K, T)) * np.random.uniform(0.3, 1.7, (1, T)) / fk[:, None], "e4m3")
    wbp = pack_weight(n((K, N)) * 1 / np.sqrt(K) * fk[:, None], "e2m1")
    return {
        "xt_words": xtp[0],
        "xt_scales": xtp[1],
        "wa": (n((K, N)) * 1 / np.sqrt(K) * fk[:, None]).astype(np.float32),
        "wb_words": wbp[0],
        "wb_scales": wbp[1],
        "bi": (1.0 * n((1, N))).astype(np.float32),
        "offs": striped(idx),
        "offs2": striped(idx2),
    }


def reference(xt_words, xt_scales, wa, wb_words, wb_scales, bi, offs, offs2):
    idx = unstriped(offs)
    idx2 = unstriped(offs2)
    xtu = unpack_weight(xt_words, xt_scales, "e4m3")
    wbu = unpack_weight(wb_words, wb_scales, "e2m1")
    xtidxg = xtu[:, idx]
    waq = mxq(f64(wa), 0, "e4m3")
    a = xtidxg.T @ waq
    xtidx2g = xtu[:, idx2]
    b0 = xtidx2g.T @ wbu
    b = b0 + f64(bi)
    s = np.tanh(2.0 * np.mean((a + f64(bi)) * b, axis=1, keepdims=True))
    y = a + s * b
    return y

@@ -1,0 +1,177 @@
+from contextlib import ExitStack
+
+import concourse.mybir as mybir
+from concourse.masks import make_identity
+
+K, T, J, N = 1024, 2048, 512, 512
+FLOPS = 2 * 2 * K * J * N
+
+F32 = mybir.dt.float32
+BF16 = mybir.dt.bfloat16
+I32 = mybir.dt.int32
+U32 = mybir.dt.uint32
+U16 = mybir.dt.uint16
+U8 = mybir.dt.uint8
+FP8X4 = mybir.dt.float8_e4m3fn_x4
+FP4X4 = mybir.dt.float4_e2m1fn_x4
+ALU = mybir.AluOpType
+ACT = mybir.ActivationFunctionType
+
+P = 128
+PACK = 4
+PASSES = K // (P * PACK)
+QUADS = 4
+ROWS = 4
+SLOT_TILES = J // P
+MOVED = 112
+HALVES = 2
+HALF = N // HALVES
+
+
+def tile_moe_experts_by_agreement_kernel(tc, xt_words, xt_scales, wa, wb_words, wb_scales, bi, offs, offs2, out):
+    nc = tc.nc
+    with ExitStack() as ctx:
+        keep = ctx.enter_context(tc.tile_pool(name="keep", bufs=1))
+        psum = ctx.enter_context(tc.psum_pool(name="psum", bufs=1))
+
+        agree = keep.tile([P, SLOT_TILES], F32, name="agree")
+        zero = keep.tile([P, 1], F32, name="zero")
+        nc.gpsimd.memset(zero[:], 0.0)
+        nc.scalar.activation(agree[:, 0:1], zero[:], ACT.Tanh)
+        list_a = keep.tile([P, J // 16], U16, name="list_a")
+        list_b = keep.tile([P, J // 16], U16, name="list_b")
+        x_scales = keep.tile([P, T], U8, name="x_scales", align_bytes=64)
+        nc.vector.memset(x_scales[:, : T // 2].bitcast(I32), 0)
+        nc.gpsimd.memset(x_scales[:, T // 2 :].bitcast(I32), 0)
+        nc.sync.dma_start(list_b[:], offs2)
+        nc.sync.dma_start(list_a[:], offs)
+        bias_cols = keep.tile([P, N // P], F32, name="bias_cols")
+        nc.sync.dma_start(bias_cols[:], bi.rearrange("o (p c) -> p (o c)", p=P))
+        for q in range(QUADS):
+            nc.sync.dma_start(
+                x_scales[32 * q : 32 * q + PASSES * ROWS, :].bitcast(I32),
+                xt_scales[:, ROWS * q : ROWS * (q + 1), :].bitcast(I32),
+            )
+        x_words = []
+        for z in range(PASSES):
+            words = keep.tile([P, T], I32, name="x_words%d" % z, align_bytes=64)
+            nc.sync.dma_start(words[:], xt_words[z].rearrange("p c r -> p (c r)").bitcast(I32))
+            x_words.append(words)
+
+        wb_codes = keep.tile([P, PASSES, 2 * N], U8, name="wb_codes", align_bytes=64)
+        wb_planes = keep.tile([P, PASSES, N], U8, name="wb_planes", align_bytes=64)
+        for q in range(QUADS):
+            nc.sync.dma_start(
+                wb_planes[32 * q : 32 * q + ROWS, :, :].bitcast(I32),
+                wb_scales[:, ROWS * q : ROWS * (q + 1), :].rearrange("z r n -> r z n").bitcast(I32),
+            )
+        nc.sync.dma_start(wb_codes[:].bitcast(I32), wb_words.rearrange("z p c -> p z c").bitcast(I32))
+
+        wa_raw = {}
+        for z in range(PASSES):
+            rows = wa[z * P * PACK : (z + 1) * P * PACK, :].rearrange("(p t) n -> p t n", t=PACK)
+            for h in range(HALVES):
+                raw = keep.tile([P, PACK, HALF], F32, name="wa_raw%d%d" % (z, h))
+                nc.sync.dma_start(raw[:], rows[:, :, h * HALF : (h + 1) * HALF])
+                wa_raw[z, h] = raw
+
+        identity = keep.tile([P, P], F32, name="identity")
+        make_identity(nc, identity[:])
+
+        bias_ps = psum.tile([P, N // P, P], F32, name="bias_ps", tag="a%d" % (SLOT_TILES - 1))
+        for c in range(N // P):
+            nc.tensor.transpose(bias_ps[:, c, :], bias_cols[:, c : c + 1].to_broadcast([P, P]), identity[:])
+        bias = keep.tile([P, N], F32, name="bias")
+        nc.scalar.copy(bias[:].rearrange("q (p c) -> q p c", c=N // P), bias_ps[:].rearrange("q c p -> q p c"))
+
+        xb_scales = keep.tile([P, J], U8, name="xb_scales", align_bytes=64)
+        nc.vector.tensor_copy(xb_scales[:], x_scales[:].indirect(list_b[:]))
+        xb_moved = keep.tile([P, J], U8, name="xb_moved", align_bytes=64)
+        nc.scalar.dma_start(xb_moved[:MOVED, :].bitcast(I32), xb_scales[ROWS : ROWS + MOVED, :].bitcast(I32))
+        xa_scales = keep.tile([P, J], U8, name="xa_scales", align_bytes=64)
+        nc.vector.tensor_copy(xa_scales[:], x_scales[:].indirect(list_a[:]))
+        xa_words = [keep.tile([P, J], U32, name="xa_words%d" % z, align_bytes=64) for z in range(PASSES)]
+        xb_words = [keep.tile([P, J], U32, name="xb_words%d" % z, align_bytes=64) for z in range(PASSES)]
+        for z in range(PASSES):
+            nc.vector.tensor_copy(xb_words[z][:], x_words[z][:].bitcast(U32).indirect(list_b[:]))
+        for z in range(PASSES):
+            nc.vector.tensor_copy(xa_words[z][:], x_words[z][:].bitcast(U32).indirect(list_a[:]))
+
+        xb_planes = [xb_scales, xb_moved]
+        b_ps = [psum.tile([P, N], F32, name="b_ps%d" % i, tag="b%d" % i) for i in range(SLOT_TILES)]
+        for z in range(PASSES):
+            for i in range(SLOT_TILES):
+                slots = slice(i * P, (i + 1) * P)
+                nc.tensor.matmul_mx(
+                    out=b_ps[i][:],
+                    lhsT=xb_words[z][:, slots].bitcast(FP8X4),
+                    lhsT_scale=xb_planes[z][:, slots],
+                    rhs=wb_codes[:, z, :].bitcast(FP4X4),
+                    rhs_scale=wb_planes[:, z, :],
+                    start=(z == 0),
+                    stop=(z == PASSES - 1),
+                )
+        bias_dot = keep.tile([P, SLOT_TILES], F32, name="bias_dot")
+        a_dot = keep.tile([P, SLOT_TILES], F32, name="a_dot")
+        b_rows = []
+        for i in range(SLOT_TILES):
+            b_row = keep.tile([P, N], F32, name="b_row%d" % i)
+            nc.vector.tensor_tensor(b_row[:], b_ps[i][:], bias[:], ALU.add)
+            b_rows.append(b_row)
+        results = [keep.tile([P, N], F32, name="result%d" % i) for i in range(SLOT_TILES)]
+        for i in range(SLOT_TILES):
+            nc.vector.scalar_tensor_tensor(
+                results[i][:], b_rows[i][:], 2.0 / N, bias[:], ALU.mult, ALU.mult, accum_out=bias_dot[:, i : i + 1]
+            )
+
+        wa_codes, wa_planes, groups = [], [], []
+        for z in range(PASSES):
+            codes = keep.tile([P, N], U32, name="wa_codes%d" % z, align_bytes=64)
+            plane = keep.tile([P, N], U8, name="wa_plane%d" % z, align_bytes=64)
+            for h in range(HALVES):
+                cols = slice(h * HALF, (h + 1) * HALF)
+                grouped = keep.tile([P, HALF, PACK], BF16, name="wa_grouped%d%d" % (z, h), align_bytes=64)
+                groups.append(grouped)
+                nc.scalar.copy(
+                    grouped[:].rearrange("p (c i) t -> p c t i", i=4),
+                    wa_raw[z, h][:].rearrange("p t (c i) -> p c t i", i=4),
+                )
+                nc.vector.quantize_mx(
+                    out=codes[:, cols].bitcast(FP8X4),
+                    scales=plane[:, cols],
+                    in_=grouped[:].rearrange("p n t -> p (n t)"),
+                )
+            wa_codes.append(codes)
+            wa_planes.append(plane)
+
+        a_ps = [psum.tile([P, N], F32, name="a_ps%d" % i, tag="a%d" % i) for i in range(SLOT_TILES)]
+        for z in range(PASSES):
+            for i in range(SLOT_TILES):
+                slots = slice(i * P, (i + 1) * P)
+                nc.tensor.matmul_mx(
+                    out=a_ps[i][:],
+                    lhsT=xa_words[z][:, slots].bitcast(FP8X4),
+                    lhsT_scale=xa_scales[ROWS * z :, slots],
+                    rhs=wa_codes[z][:].bitcast(FP8X4),
+                    rhs_scale=wa_planes[z][:],
+                    start=(z == 0),
+                    stop=(z == PASSES - 1),
+                )
+
+        def dot(i):
+            nc.vector.scalar_tensor_tensor(
+                results[i][:], a_ps[i][:], 2.0 / N, b_rows[i][:], ALU.mult, ALU.mult, accum_out=a_dot[:, i : i + 1]
+            )
+            nc.scalar.activation(agree[:, i : i + 1], a_dot[:, i : i + 1], ACT.Tanh, bias=bias_dot[:, i : i + 1])
+
+        def combine(i):
+            nc.vector.scalar_tensor_tensor(
+                results[i][:], b_rows[i][:], agree[:, i : i + 1], a_ps[i][:], ALU.mult, ALU.add
+            )
+            nc.sync.dma_start(out[i * P : (i + 1) * P, :], results[i][:])
+
+        dot(0)
+        for i in range(1, SLOT_TILES):
+            dot(i)
+            combine(i - 1)
+        combine(SLOT_TILES - 1)

@@ -52,25 +52,23 @@ def tile_moe_experts_by_agreement_kernel(tc, xt_words, xt_scales, wa, wb_words, 
                 x_scales[32 * q : 32 * q + PASSES * ROWS, :].bitcast(I32),
                 xt_scales[:, ROWS * q : ROWS * (q + 1), :].bitcast(I32),
             )
-        x_words = []
-        for z in range(PASSES):
-            words = keep.tile([P, T], I32, name="x_words%d" % z, align_bytes=64)
-            nc.sync.dma_start(words[:], xt_words[z].rearrange("p c r -> p (c r)").bitcast(I32))
-            x_words.append(words)
-
-        wb_codes = keep.tile([P, PASSES, 2 * N], U8, name="wb_codes", align_bytes=64)
+        x_words = [keep.tile([P, T], I32, name="x_words%d" % z, align_bytes=64) for z in range(PASSES)]
+        nc.sync.dma_start(x_words[0][:], xt_words[0].rearrange("p c r -> p (c r)").bitcast(I32))
         wb_planes = keep.tile([P, PASSES, N], U8, name="wb_planes", align_bytes=64)
         for q in range(QUADS):
             nc.sync.dma_start(
                 wb_planes[32 * q : 32 * q + ROWS, :, :].bitcast(I32),
                 wb_scales[:, ROWS * q : ROWS * (q + 1), :].rearrange("z r n -> r z n").bitcast(I32),
             )
+
+        wb_codes = keep.tile([P, PASSES, 2 * N], U8, name="wb_codes", align_bytes=64)
         nc.sync.dma_start(wb_codes[:].bitcast(I32), wb_words.rearrange("z p c -> p z c").bitcast(I32))
+        nc.sync.dma_start(x_words[1][:], xt_words[1].rearrange("p c r -> p (c r)").bitcast(I32))
 
         wa_raw = {}
-        for z in range(PASSES):
-            rows = wa[z * P * PACK : (z + 1) * P * PACK, :].rearrange("(p t) n -> p t n", t=PACK)
-            for h in range(HALVES):
+        for h in range(HALVES):
+            for z in range(PASSES):
+                rows = wa[z * P * PACK : (z + 1) * P * PACK, :].rearrange("(p t) n -> p t n", t=PACK)
                 raw = keep.tile([P, PACK, HALF], F32, name="wa_raw%d%d" % (z, h))
                 nc.sync.dma_start(raw[:], rows[:, :, h * HALF : (h + 1) * HALF])
                 wa_raw[z, h] = raw
@@ -97,6 +95,22 @@ def tile_moe_experts_by_agreement_kernel(tc, xt_words, xt_scales, wa, wb_words, 
         for z in range(PASSES):
             nc.vector.tensor_copy(xa_words[z][:], x_words[z][:].bitcast(U32).indirect(list_a[:]))
 
+        wa_codes, wa_planes = {}, {}
+        for h in range(HALVES):
+            for z in range(PASSES):
+                grouped = keep.tile([P, HALF, PACK], BF16, name="wa_grouped%d%d" % (z, h), align_bytes=64)
+                nc.scalar.copy(
+                    grouped[:].rearrange("p (c i) t -> p c t i", i=4),
+                    wa_raw[z, h][:].rearrange("p t (c i) -> p c t i", i=4),
+                )
+                codes = keep.tile([P, HALF], U32, name="wa_codes%d%d" % (z, h), align_bytes=64)
+                plane = keep.tile([P, HALF], U8, name="wa_plane%d%d" % (z, h), align_bytes=64)
+                nc.vector.quantize_mx(
+                    out=codes[:].bitcast(FP8X4), scales=plane[:], in_=grouped[:].rearrange("p n t -> p (n t)")
+                )
+                wa_codes[z, h] = codes
+                wa_planes[z, h] = plane
+
         xb_planes = [xb_scales, xb_moved]
         b_ps = [psum.tile([P, N], F32, name="b_ps%d" % i, tag="b%d" % i) for i in range(SLOT_TILES)]
         for z in range(PASSES):
@@ -119,48 +133,48 @@ def tile_moe_experts_by_agreement_kernel(tc, xt_words, xt_scales, wa, wb_words, 
             nc.vector.tensor_tensor(b_row[:], b_ps[i][:], bias[:], ALU.add)
             b_rows.append(b_row)
         results = [keep.tile([P, N], F32, name="result%d" % i) for i in range(SLOT_TILES)]
+        products = [keep.tile([P, N + HALF], F32, name="product%d" % i) for i in range(SLOT_TILES)]
         for i in range(SLOT_TILES):
-            nc.vector.scalar_tensor_tensor(
-                results[i][:], b_rows[i][:], 2.0 / N, bias[:], ALU.mult, ALU.mult, accum_out=bias_dot[:, i : i + 1]
-            )
-
-        wa_codes, wa_planes, groups = [], [], []
-        for z in range(PASSES):
-            codes = keep.tile([P, N], U32, name="wa_codes%d" % z, align_bytes=64)
-            plane = keep.tile([P, N], U8, name="wa_plane%d" % z, align_bytes=64)
             for h in range(HALVES):
                 cols = slice(h * HALF, (h + 1) * HALF)
-                grouped = keep.tile([P, HALF, PACK], BF16, name="wa_grouped%d%d" % (z, h), align_bytes=64)
-                groups.append(grouped)
-                nc.scalar.copy(
-                    grouped[:].rearrange("p (c i) t -> p c t i", i=4),
-                    wa_raw[z, h][:].rearrange("p t (c i) -> p c t i", i=4),
-                )
-                nc.vector.quantize_mx(
-                    out=codes[:, cols].bitcast(FP8X4),
-                    scales=plane[:, cols],
-                    in_=grouped[:].rearrange("p n t -> p (n t)"),
-                )
-            wa_codes.append(codes)
-            wa_planes.append(plane)
+                nc.gpsimd.tensor_tensor(products[i][:, cols], b_rows[i][:, cols], bias[:, cols], ALU.mult)
 
         a_ps = [psum.tile([P, N], F32, name="a_ps%d" % i, tag="a%d" % i) for i in range(SLOT_TILES)]
-        for z in range(PASSES):
-            for i in range(SLOT_TILES):
-                slots = slice(i * P, (i + 1) * P)
-                nc.tensor.matmul_mx(
-                    out=a_ps[i][:],
-                    lhsT=xa_words[z][:, slots].bitcast(FP8X4),
-                    lhsT_scale=xa_scales[ROWS * z :, slots],
-                    rhs=wa_codes[z][:].bitcast(FP8X4),
-                    rhs_scale=wa_planes[z][:],
-                    start=(z == 0),
-                    stop=(z == PASSES - 1),
-                )
+        for h in range(HALVES):
+            cols = slice(h * HALF, (h + 1) * HALF)
+            for z in range(PASSES):
+                for i in range(SLOT_TILES):
+                    slots = slice(i * P, (i + 1) * P)
+                    nc.tensor.matmul_mx(
+                        out=a_ps[i][:, cols],
+                        lhsT=xa_words[z][:, slots].bitcast(FP8X4),
+                        lhsT_scale=xa_scales[ROWS * z :, slots],
+                        rhs=wa_codes[z, h][:].bitcast(FP8X4),
+                        rhs_scale=wa_planes[z, h][:],
+                        start=(z == 0),
+                        stop=(z == PASSES - 1),
+                    )
+            if h == 0:
+                for i in range(SLOT_TILES):
+                    nc.vector.tensor_tensor(products[i][:, N:], a_ps[i][:, cols], b_rows[i][:, cols], ALU.mult)
+
+        spent = wa_raw[PASSES - 1, HALVES - 1][:].rearrange("p t n -> p (t n)")
+        last = slice(HALF, N)
+
+        for i in range(SLOT_TILES):
+            nc.scalar.activation(
+                spent[:, : N + HALF], products[i][:], ACT.Copy, scale=2.0 / N, accum_out=bias_dot[:, i : i + 1]
+            )
 
         def dot(i):
             nc.vector.scalar_tensor_tensor(
-                results[i][:], a_ps[i][:], 2.0 / N, b_rows[i][:], ALU.mult, ALU.mult, accum_out=a_dot[:, i : i + 1]
+                results[i][:, last],
+                a_ps[i][:, last],
+                2.0 / N,
+                b_rows[i][:, last],
+                ALU.mult,
+                ALU.mult,
+                accum_out=a_dot[:, i : i + 1],
             )
             nc.scalar.activation(agree[:, i : i + 1], a_dot[:, i : i + 1], ACT.Tanh, bias=bias_dot[:, i : i + 1])
 

from contextlib import ExitStack

import concourse.mybir as mybir
from concourse.masks import make_identity

K, T, J, N = 1024, 2048, 512, 512
FLOPS = 2 * 2 * K * J * N

F32 = mybir.dt.float32
BF16 = mybir.dt.bfloat16
I32 = mybir.dt.int32
U32 = mybir.dt.uint32
U16 = mybir.dt.uint16
U8 = mybir.dt.uint8
FP8X4 = mybir.dt.float8_e4m3fn_x4
FP4X4 = mybir.dt.float4_e2m1fn_x4
ALU = mybir.AluOpType
ACT = mybir.ActivationFunctionType

P = 128
PACK = 4
PASSES = K // (P * PACK)
QUADS = 4
ROWS = 4
SLOT_TILES = J // P
MOVED = 112
HALVES = 2
HALF = N // HALVES


def tile_moe_experts_by_agreement_kernel(tc, xt_words, xt_scales, wa, wb_words, wb_scales, bi, offs, offs2, out):
    nc = tc.nc
    with ExitStack() as ctx:
        keep = ctx.enter_context(tc.tile_pool(name="keep", bufs=1))
        psum = ctx.enter_context(tc.psum_pool(name="psum", bufs=1))

        agree = keep.tile([P, SLOT_TILES], F32, name="agree")
        zero = keep.tile([P, 1], F32, name="zero")
        nc.gpsimd.memset(zero[:], 0.0)
        nc.scalar.activation(agree[:, 0:1], zero[:], ACT.Tanh)
        list_a = keep.tile([P, J // 16], U16, name="list_a")
        list_b = keep.tile([P, J // 16], U16, name="list_b")
        x_scales = keep.tile([P, T], U8, name="x_scales", align_bytes=64)
        nc.vector.memset(x_scales[:, : T // 2].bitcast(I32), 0)
        nc.gpsimd.memset(x_scales[:, T // 2 :].bitcast(I32), 0)
        nc.sync.dma_start(list_b[:], offs2)
        nc.sync.dma_start(list_a[:], offs)
        bias_cols = keep.tile([P, N // P], F32, name="bias_cols")
        nc.sync.dma_start(bias_cols[:], bi.rearrange("o (p c) -> p (o c)", p=P))
        for q in range(QUADS):
            nc.sync.dma_start(
                x_scales[32 * q : 32 * q + PASSES * ROWS, :].bitcast(I32),
                xt_scales[:, ROWS * q : ROWS * (q + 1), :].bitcast(I32),
            )
        x_words = [keep.tile([P, T], I32, name="x_words%d" % z, align_bytes=64) for z in range(PASSES)]
        nc.sync.dma_start(x_words[0][:], xt_words[0].rearrange("p c r -> p (c r)").bitcast(I32))
        wb_planes = keep.tile([P, PASSES, N], U8, name="wb_planes", align_bytes=64)
        for q in range(QUADS):
            nc.sync.dma_start(
                wb_planes[32 * q : 32 * q + ROWS, :, :].bitcast(I32),
                wb_scales[:, ROWS * q : ROWS * (q + 1), :].rearrange("z r n -> r z n").bitcast(I32),
            )

        wb_codes = keep.tile([P, PASSES, 2 * N], U8, name="wb_codes", align_bytes=64)
        nc.sync.dma_start(wb_codes[:].bitcast(I32), wb_words.rearrange("z p c -> p z c").bitcast(I32))
        nc.sync.dma_start(x_words[1][:], xt_words[1].rearrange("p c r -> p (c r)").bitcast(I32))

        wa_raw = {}
        for h in range(HALVES):
            for z in range(PASSES):
                rows = wa[z * P * PACK : (z + 1) * P * PACK, :].rearrange("(p t) n -> p t n", t=PACK)
                raw = keep.tile([P, PACK, HALF], F32, name="wa_raw%d%d" % (z, h))
                nc.sync.dma_start(raw[:], rows[:, :, h * HALF : (h + 1) * HALF])
                wa_raw[z, h] = raw

        identity = keep.tile([P, P], F32, name="identity")
        make_identity(nc, identity[:])

        bias_ps = psum.tile([P, N // P, P], F32, name="bias_ps", tag="a%d" % (SLOT_TILES - 1))
        for c in range(N // P):
            nc.tensor.transpose(bias_ps[:, c, :], bias_cols[:, c : c + 1].to_broadcast([P, P]), identity[:])
        bias = keep.tile([P, N], F32, name="bias")
        nc.scalar.copy(bias[:].rearrange("q (p c) -> q p c", c=N // P), bias_ps[:].rearrange("q c p -> q p c"))

        xb_scales = keep.tile([P, J], U8, name="xb_scales", align_bytes=64)
        nc.vector.tensor_copy(xb_scales[:], x_scales[:].indirect(list_b[:]))
        xb_moved = keep.tile([P, J], U8, name="xb_moved", align_bytes=64)
        nc.scalar.dma_start(xb_moved[:MOVED, :].bitcast(I32), xb_scales[ROWS : ROWS + MOVED, :].bitcast(I32))
        xa_scales = keep.tile([P, J], U8, name="xa_scales", align_bytes=64)
        nc.vector.tensor_copy(xa_scales[:], x_scales[:].indirect(list_a[:]))
        xa_words = [keep.tile([P, J], U32, name="xa_words%d" % z, align_bytes=64) for z in range(PASSES)]
        xb_words = [keep.tile([P, J], U32, name="xb_words%d" % z, align_bytes=64) for z in range(PASSES)]
        for z in range(PASSES):
            nc.vector.tensor_copy(xb_words[z][:], x_words[z][:].bitcast(U32).indirect(list_b[:]))
        for z in range(PASSES):
            nc.vector.tensor_copy(xa_words[z][:], x_words[z][:].bitcast(U32).indirect(list_a[:]))

        wa_codes, wa_planes = {}, {}
        for h in range(HALVES):
            for z in range(PASSES):
                grouped = keep.tile([P, HALF, PACK], BF16, name="wa_grouped%d%d" % (z, h), align_bytes=64)
                nc.scalar.copy(
                    grouped[:].rearrange("p (c i) t -> p c t i", i=4),
                    wa_raw[z, h][:].rearrange("p t (c i) -> p c t i", i=4),
                )
                codes = keep.tile([P, HALF], U32, name="wa_codes%d%d" % (z, h), align_bytes=64)
                plane = keep.tile([P, HALF], U8, name="wa_plane%d%d" % (z, h), align_bytes=64)
                nc.vector.quantize_mx(
                    out=codes[:].bitcast(FP8X4), scales=plane[:], in_=grouped[:].rearrange("p n t -> p (n t)")
                )
                wa_codes[z, h] = codes
                wa_planes[z, h] = plane

        xb_planes = [xb_scales, xb_moved]
        b_ps = [psum.tile([P, N], F32, name="b_ps%d" % i, tag="b%d" % i) for i in range(SLOT_TILES)]
        for z in range(PASSES):
            for i in range(SLOT_TILES):
                slots = slice(i * P, (i + 1) * P)
                nc.tensor.matmul_mx(
                    out=b_ps[i][:],
                    lhsT=xb_words[z][:, slots].bitcast(FP8X4),
                    lhsT_scale=xb_planes[z][:, slots],
                    rhs=wb_codes[:, z, :].bitcast(FP4X4),
                    rhs_scale=wb_planes[:, z, :],
                    start=(z == 0),
                    stop=(z == PASSES - 1),
                )
        bias_dot = keep.tile([P, SLOT_TILES], F32, name="bias_dot")
        a_dot = keep.tile([P, SLOT_TILES], F32, name="a_dot")
        b_rows = []
        for i in range(SLOT_TILES):
            b_row = keep.tile([P, N], F32, name="b_row%d" % i)
            nc.vector.tensor_tensor(b_row[:], b_ps[i][:], bias[:], ALU.add)
            b_rows.append(b_row)
        results = [keep.tile([P, N], F32, name="result%d" % i) for i in range(SLOT_TILES)]
        products = [keep.tile([P, N + HALF], F32, name="product%d" % i) for i in range(SLOT_TILES)]
        for i in range(SLOT_TILES):
            for h in range(HALVES):
                cols = slice(h * HALF, (h + 1) * HALF)
                nc.gpsimd.tensor_tensor(products[i][:, cols], b_rows[i][:, cols], bias[:, cols], ALU.mult)

        a_ps = [psum.tile([P, N], F32, name="a_ps%d" % i, tag="a%d" % i) for i in range(SLOT_TILES)]
        for h in range(HALVES):
            cols = slice(h * HALF, (h + 1) * HALF)
            for z in range(PASSES):
                for i in range(SLOT_TILES):
                    slots = slice(i * P, (i + 1) * P)
                    nc.tensor.matmul_mx(
                        out=a_ps[i][:, cols],
                        lhsT=xa_words[z][:, slots].bitcast(FP8X4),
                        lhsT_scale=xa_scales[ROWS * z :, slots],
                        rhs=wa_codes[z, h][:].bitcast(FP8X4),
                        rhs_scale=wa_planes[z, h][:],
                        start=(z == 0),
                        stop=(z == PASSES - 1),
                    )
            if h == 0:
                for i in range(SLOT_TILES):
                    nc.vector.tensor_tensor(products[i][:, N:], a_ps[i][:, cols], b_rows[i][:, cols], ALU.mult)

        spent = wa_raw[PASSES - 1, HALVES - 1][:].rearrange("p t n -> p (t n)")
        last = slice(HALF, N)

        for i in range(SLOT_TILES):
            nc.scalar.activation(
                spent[:, : N + HALF], products[i][:], ACT.Copy, scale=2.0 / N, accum_out=bias_dot[:, i : i + 1]
            )

        def dot(i):
            nc.vector.scalar_tensor_tensor(
                results[i][:, last],
                a_ps[i][:, last],
                2.0 / N,
                b_rows[i][:, last],
                ALU.mult,
                ALU.mult,
                accum_out=a_dot[:, i : i + 1],
            )
            nc.scalar.activation(agree[:, i : i + 1], a_dot[:, i : i + 1], ACT.Tanh, bias=bias_dot[:, i : i + 1])

        def combine(i):
            nc.vector.scalar_tensor_tensor(
                results[i][:], b_rows[i][:], agree[:, i : i + 1], a_ps[i][:], ALU.mult, ALU.add
            )
            nc.sync.dma_start(out[i * P : (i + 1) * P, :], results[i][:])

        dot(0)
        for i in range(1, SLOT_TILES):
            dot(i)
            combine(i - 1)
        combine(SLOT_TILES - 1)
